import numpy as np
import ml_dtypes


def mxq(x, axis, fmt="e4m3"):
    dtype, down = {"e4m3": (ml_dtypes.float8_e4m3fn, 7), "e5m2": (ml_dtypes.float8_e5m2, 14)}[fmt]
    v = np.moveaxis(np.asarray(x, np.float32).astype(ml_dtypes.bfloat16).astype(np.float64), axis, -1)
    blocks = v.reshape(v.shape[:-1] + (-1, 32))
    amax = np.abs(blocks).max(-1, keepdims=True)
    byte = np.maximum(np.where(amax > 0, np.frexp(amax)[1] - 1 + 127, 0) - down, 1)
    scale = np.exp2(byte - 127.0)
    codes = (blocks / scale).astype(np.float32).astype(dtype).astype(np.float64)
    return np.moveaxis((codes * scale).reshape(v.shape), -1, axis)


WIDE = False


def mx_kscale(k):
    if not WIDE:
        return np.ones(k)
    levels = np.array([10, -10, 5, -5, 0])
    if k % 512:
        return np.exp2(np.random.permutation(np.resize(levels, k // 32))).repeat(32)
    a = np.empty((k // 512, 16))
    for p in range(k // 512):
        a[p, :8] = np.random.permutation(np.resize(levels, 8))
        for g in range(8):
            far = levels[np.abs(levels - a[p, g]) >= 10]
            a[p, g + 8] = far[np.random.randint(len(far))]
    return np.exp2(a.ravel()).repeat(32)


def f64(x):
    return np.asarray(x).astype(np.float64)


def striped(idx):
    return np.tile(idx.reshape(-1, 16).T, (8, 1)).astype(np.uint16)


def unstriped(offs):
    return offs[:16].T.reshape(-1).astype(np.int64)


def pack_weight(w):
    k, n = w.shape
    w = f64(np.asarray(w, np.float32).astype(ml_dtypes.bfloat16)).reshape(k // 32, 32, n)
    amax = np.abs(w).max(1)
    byte = np.clip(np.where(amax > 0, np.frexp(amax)[1] - 1 + 127 - 7, 1), 1, 254)
    scaled = (w * np.exp2(127.0 - byte)[:, None, :]).reshape(k, n).astype(np.float32)
    words = np.ascontiguousarray(scaled.reshape(k // 512, 128, 4, n).transpose(0, 1, 3, 2)).astype(ml_dtypes.float8_e4m3fn).view(np.uint8)
    return words, np.ascontiguousarray(byte.astype(np.uint8).reshape(k // 512, 16, n))


def unpack_weight(words, scales):
    g, p, n, _ = words.shape
    vals = np.ascontiguousarray(words).view(ml_dtypes.float8_e4m3fn).astype(np.float64) * np.repeat(np.exp2(scales.astype(np.float64) - 127.0), 8, axis=1)[..., None]
    return vals.transpose(0, 1, 3, 2).reshape(g * 512, n)


def planes(y):
    n, m = y.shape
    v = y.astype(np.float32).astype(ml_dtypes.bfloat16).astype(np.float64).reshape(n // 32, 32, m)
    top = np.abs(v).max(1)
    byte = np.clip(np.where(top > 0, np.frexp(top)[1] - 1 + 127 - 7, 1), 1, 254)
    codes = (v * np.exp2(127.0 - byte)[:, None, :]).reshape(n, m).astype(np.float32).astype(ml_dtypes.float8_e4m3fn).view(np.uint8)
    words = codes.reshape(n // 512, 128, 4, m).transpose(0, 1, 3, 2)
    return np.ascontiguousarray(words), np.ascontiguousarray(byte.astype(np.uint8).reshape(n // 512, 16, m))


def relu(v):
    return np.maximum(v, 0.0)


K, T, S, D, H, N = 512, 1024, 512, 8, 512, 512


def setup_inputs():
    n = np.random.standard_normal
    s = mx_kscale(K)[:, None]
    u = mx_kscale(H)
    packed_xT = pack_weight(n((K, T)) * s)
    return {
        "x_words": packed_xT[0],
        "x_scales": packed_xT[1],
        "wc": (n((K, N)) / np.sqrt(K) / s).astype(np.float32),
        "ws": (n((K, N)) / np.sqrt(K) / s).astype(np.float32),
        "unit": (np.random.uniform(0.5, 1.0, (H, 1)) * u[:, None]).astype(np.float32),
        "vc": (n((H, N)) / np.sqrt(2 * H) / u[:, None]).astype(np.float32),
        "vs": (n((H, N)) / np.sqrt(2 * H) / u[:, None]).astype(np.float32),
        "offs": striped(np.random.permutation(T)[:S]),
    }


def reference(x_words, x_scales, wc, ws, unit, vc, vs, offs):
    xq = unpack_weight(x_words, x_scales)[:, unstriped(offs)]
    re = mxq(f64(wc), 0, "e4m3").T @ xq
    im = mxq(f64(ws), 0, "e4m3").T @ xq
    pw = (re) ** 2 + (im) ** 2
    nf = 1.5 * (pw.reshape(len(pw), -1, D).min(axis=2))
    gain = np.sqrt(relu(-1.0 * (np.repeat(nf, D, axis=1) / (pw + 0.05)) + 1.0) + 0.02)
    zvc = f64(unit) * (gain * re)
    zvs = f64(unit) * (gain * im)
    out_0 = mxq(f64(vc), 0, "e4m3").T @ mxq(zvc, 0, "e4m3") + mxq(f64(vs), 0, "e4m3").T @ mxq(zvs, 0, "e4m3")
    return (out_0,) + planes(out_0)

@@ -1,0 +1,225 @@
+from contextlib import ExitStack
+
+import concourse.mybir as mybir
+
+K, T, S, D, H, N = 512, 1024, 512, 8, 512, 512
+FLOPS = 4 * 2 * 512 * 512 * 512
+
+F32 = mybir.dt.float32
+BF16 = mybir.dt.bfloat16
+I32 = mybir.dt.int32
+U32 = mybir.dt.uint32
+U16 = mybir.dt.uint16
+U8 = mybir.dt.uint8
+FP8X4 = mybir.dt.float8_e4m3fn_x4
+ALU = mybir.AluOpType
+ACT = mybir.ActivationFunctionType
+
+P = 128
+PACK = 4
+CH = 128
+NCH = S // CH
+HALF = 256
+
+
+def tile_picked_ysubtr_sub_po_kernel(tc, x_words, x_scales, wc, ws, unit, vc, vs, offs, out_0, out_1, out_2):
+    nc = tc.nc
+    with ExitStack() as ctx:
+        keep = ctx.enter_context(tc.tile_pool(name="keep", bufs=1))
+        psum = ctx.enter_context(tc.psum_pool(name="psum", bufs=1))
+
+        xs = keep.tile([P, T], U8, name="xs", align_bytes=64)
+        nc.gpsimd.memset(xs[:].bitcast(I32), 0)
+        offsets = keep.tile([P, S // 16], U16, name="offsets")
+        nc.sync.dma_start(offsets[:], offs)
+        xw = keep.tile([P, T], I32, name="xw", align_bytes=64)
+        nc.sync.dma_start(out=xw[:], in_=x_words[0].rearrange("p n t -> p (n t)").bitcast(I32))
+        for q in range(4):
+            nc.scalar.dma_start(out=xs[32 * q : 32 * q + 4, :].bitcast(I32), in_=x_scales[0, 4 * q : 4 * q + 4, :].bitcast(I32))
+
+        warm = keep.tile([P, 2], F32, name="warm")
+        nc.gpsimd.memset(warm[:, 0:1], 1.0)
+        nc.scalar.activation(warm[:, 1:2], warm[:, 0:1], ACT.Abs_reciprocal_sqrt)
+
+        def load(w, name, slot):
+            halves = []
+            for h in range(2):
+                raw = keep.tile([P, PACK, HALF], F32, name=f"{name}_raw{h}", tag=f"raw{slot}{h}")
+                nc.sync.dma_start(out=raw[:], in_=w.rearrange("(p j) c -> p j c", j=PACK)[:, :, h * HALF : (h + 1) * HALF])
+                halves.append(raw)
+            return halves
+
+        wc_raw = load(wc, "wc", 0)
+        ws_raw = load(ws, "ws", 1)
+        unit_sb = keep.tile([P, PACK], F32, name="unit_sb")
+        nc.gpsimd.dma_start(out=unit_sb[:], in_=unit.rearrange("(p t) o -> p (t o)", t=PACK))
+
+        xg = keep.tile([P, S], U32, name="xg", align_bytes=64)
+        xgs = keep.tile([P, S], U8, name="xgs", align_bytes=64)
+        nc.vector.tensor_copy(xg[:], xw[:].bitcast(U32).indirect(offsets[:]))
+        nc.vector.tensor_copy(xgs[:], xs[:].indirect(offsets[:]))
+
+        def deal(copy, grouped, raws, part):
+            h, m0 = part // 2, 32 * (part % 2)
+            copy(
+                out=grouped[:, :, 32 * part : 32 * (part + 1), :].rearrange("p t m j -> p m j t"),
+                in_=raws[h][:].rearrange("p j (m t) -> p m j t", t=PACK)[:, m0 : m0 + 32, :, :],
+            )
+
+        def forward_weights(name, raws, copies):
+            codes = keep.tile([P, PACK, P], U32, name=f"{name}_codes", align_bytes=64)
+            scales = keep.tile([P, PACK, P], U8, name=f"{name}_scales", align_bytes=64)
+            for h in range(2):
+                grouped = keep.tile([P, PACK, 64, PACK], BF16, name=f"{name}_g{h}", align_bytes=64)
+                for u in range(2):
+                    copies[2 * h + u](
+                        out=grouped[:, :, 32 * u : 32 * (u + 1), :].rearrange("p t m j -> p m j t"),
+                        in_=raws[h][:].rearrange("p j (m t) -> p m j t", t=PACK)[:, 32 * u : 32 * (u + 1), :, :],
+                    )
+                for t in range(PACK):
+                    nc.vector.quantize_mx(
+                        out=codes[:, t, 64 * h : 64 * (h + 1)].bitcast(FP8X4),
+                        scales=scales[:, t, 64 * h : 64 * (h + 1)],
+                        in_=grouped[:, t, :, :].rearrange("p m j -> p (m j)"),
+                    )
+            return codes[:].rearrange("p t m -> p (t m)"), scales[:].rearrange("p t m -> p (t m)")
+
+        def quantise(name, grouped):
+            codes = keep.tile([P, N], U32, name=f"{name}_codes", align_bytes=64)
+            scales = keep.tile([P, N], U8, name=f"{name}_scales", align_bytes=64)
+            nc.vector.quantize_mx(out=codes[:].bitcast(FP8X4), scales=scales[:], in_=grouped[:].rearrange("p t m j -> p (t m j)"))
+            return codes[:], scales[:]
+
+        def product(bank, t, weights, codes, scales, start, stop):
+            cols = slice(t * P, (t + 1) * P)
+            nc.tensor.matmul_mx(
+                out=bank[:, t, :],
+                lhsT=weights[0][:, cols].bitcast(FP8X4),
+                lhsT_scale=weights[1][:, cols],
+                rhs=codes.bitcast(FP8X4),
+                rhs_scale=scales,
+                start=start,
+                stop=stop,
+            )
+
+        on_v, on_s = nc.vector.tensor_copy, nc.scalar.copy
+        wc_q = forward_weights("wc", wc_raw, (on_s, on_v, on_s, on_v))
+
+        re, re2 = [], []
+        for c in range(NCH):
+            cols = slice(c * CH, (c + 1) * CH)
+            bank = psum.tile([P, PACK, CH], F32, name=f"re{c}", tag=f"a{c}")
+            for t in range(PACK):
+                product(bank, t, wc_q, xg[:, cols], xgs[:, cols], True, True)
+            sq = keep.tile([P, PACK * CH], F32, name=f"re2_{c}")
+            nc.scalar.activation(sq[:], bank[:].rearrange("p t j -> p (t j)"), ACT.Square)
+            re.append(bank)
+            re2.append(sq)
+
+        ws_q = forward_weights("ws", ws_raw, (on_v, on_v, on_v, on_v))
+
+        vc_raw = load(vc, "vc", 0)
+        vs_raw = load(vs, "vs", 1)
+
+        im, pw, least, inv, floor2, gain, zq = {}, {}, {}, {}, {}, {}, {}
+
+        def power(c):
+            cols = slice(c * CH, (c + 1) * CH)
+            im[c] = psum.tile([P, PACK, CH], F32, name=f"im{c}", tag=f"b{c}")
+            for t in range(PACK):
+                product(im[c], t, ws_q, xg[:, cols], xgs[:, cols], True, True)
+            im2 = keep.tile([P, PACK * CH], F32, name=f"im2_{c}")
+            nc.scalar.activation(im2[:], im[c][:].rearrange("p t j -> p (t j)"), ACT.Square)
+            pw[c] = keep.tile([P, PACK * CH], F32, name=f"pw{c}")
+            nc.vector.tensor_tensor(pw[c][:], re2[c][:], im2[:], ALU.add)
+
+        def noise(c):
+            least[c] = keep.tile([P, PACK * CH // D], F32, name=f"least{c}")
+            nc.vector.tensor_reduce(least[c][:], pw[c][:].rearrange("p (v d) -> p v d", d=D), mybir.AxisListType.X, ALU.min)
+            root = keep.tile([P, PACK * CH], F32, name=f"root{c}")
+            nc.scalar.activation(root[:], pw[c][:], ACT.Abs_reciprocal_sqrt, bias=0.05)
+            inv[c] = keep.tile([P, PACK * CH], F32, name=f"inv{c}")
+            nc.scalar.activation(inv[c][:], root[:], ACT.Square)
+
+        def squared_gain(c):
+            ratio = keep.tile([P, PACK * CH // D, D], F32, name=f"ratio{c}")
+            nc.vector.scalar_tensor_tensor(
+                ratio[:],
+                inv[c][:].rearrange("p (v d) -> p v d", d=D),
+                -1.5,
+                least[c][:].unsqueeze(2).broadcast_to([P, PACK * CH // D, D]),
+                ALU.mult,
+                ALU.mult,
+            )
+            floor2[c] = keep.tile([P, PACK, CH], F32, name=f"g2_{c}")
+            nc.vector.tensor_scalar(
+                floor2[c][:].rearrange("p t j -> p (t j)"), ratio[:].rearrange("p v d -> p (v d)"), 1.02, 0.02, ALU.add, ALU.max
+            )
+
+        def weighted_gain(c):
+            rs = keep.tile([P, PACK, CH], F32, name=f"rs{c}")
+            nc.scalar.activation(rs[:], floor2[c][:], ACT.Abs_reciprocal_sqrt)
+            gain[c] = keep.tile([P, PACK, CH], F32, name=f"gain{c}")
+            for t in range(PACK):
+                nc.vector.scalar_tensor_tensor(gain[c][:, t, :], floor2[c][:, t, :], unit_sb[:, t : t + 1], rs[:, t, :], ALU.mult, ALU.mult)
+
+        def hidden(c):
+            z = keep.tile([P, 2, CH, PACK], BF16, name=f"z{c}", align_bytes=64)
+            for u, bank in enumerate((re[c], im[c])):
+                nc.vector.tensor_tensor(
+                    z[:, u, :, :].rearrange("p (a i) t -> p a t i", i=4),
+                    bank[:].rearrange("p t (a i) -> p a t i", i=4),
+                    gain[c][:].rearrange("p t (a i) -> p a t i", i=4),
+                    ALU.mult,
+                )
+            codes = keep.tile([P, 2, CH], U32, name=f"z_codes{c}", align_bytes=64)
+            scales = keep.tile([P, 2, CH], U8, name=f"z_scales{c}", align_bytes=64)
+            nc.vector.quantize_mx(
+                out=codes[:].rearrange("p u j -> p (u j)").bitcast(FP8X4),
+                scales=scales[:].rearrange("p u j -> p (u j)"),
+                in_=z[:].rearrange("p u j t -> p (u j t)"),
+            )
+            zq[c] = (codes, scales)
+
+        y_codes = keep.tile([P, S], U32, name="y_codes", align_bytes=64)
+        y_scales = keep.tile([P, S], U8, name="y_scales", align_bytes=64)
+        out_rows = out_0.rearrange("(p t) j -> p t j", t=PACK)
+        out_words = out_1[0].rearrange("p n t -> p (n t)").bitcast(I32)
+
+        def result(c, vc_q, vs_q):
+            cols = slice(c * CH, (c + 1) * CH)
+            bank = psum.tile([P, PACK, CH], F32, name=f"y{c}", tag=f"a{c}")
+            codes, scales = zq[c]
+            for t in range(PACK):
+                product(bank, t, vc_q, codes[:, 0, :], scales[:, 0, :], True, False)
+                product(bank, t, vs_q, codes[:, 1, :], scales[:, 1, :], False, True)
+            y = keep.tile([P, PACK, CH], F32, name=f"y_sb{c}")
+            nc.scalar.copy(out=y[:], in_=bank[:])
+            nc.sync.dma_start(out=out_rows[:, :, cols], in_=y[:])
+            y_g = keep.tile([P, CH, PACK], BF16, name=f"y_g{c}", align_bytes=64)
+            if c < NCH - 2:
+                on_s(out=y_g[:].rearrange("p (a i) t -> p a t i", i=4), in_=bank[:].rearrange("p t (a i) -> p a t i", i=4))
+            else:
+                on_v(out=y_g[:].rearrange("p (a i) t -> p a t i", i=4), in_=y[:].rearrange("p t (a i) -> p a t i", i=4))
+            nc.vector.quantize_mx(out=y_codes[:, cols].bitcast(FP8X4), scales=y_scales[:, cols], in_=y_g[:].rearrange("p j t -> p (j t)"))
+            nc.sync.dma_start(out=out_words[:, cols], in_=y_codes[:, cols].bitcast(I32))
+
+        vc_g = keep.tile([P, PACK, P, PACK], BF16, name="vc_g", align_bytes=64)
+        vs_g = keep.tile([P, PACK, P, PACK], BF16, name="vs_g", align_bytes=64)
+        stages = (power, noise, squared_gain, weighted_gain, hidden)
+        for step in range(NCH + len(stages) - 1):
+            for s in reversed(range(len(stages))):
+                if 0 <= step - s < NCH:
+                    stages[s](step - s)
+        for part in range(4):
+            deal(on_s, vc_g, vc_raw, part)
+        vc_q = quantise("vc", vc_g)
+        for part in range(4):
+            deal(on_s, vs_g, vs_raw, part)
+        vs_q = quantise("vs", vs_g)
+        for c in range(NCH):
+            result(c, vc_q, vs_q)
+
+        for q in range(4):
+            queue = nc.sync if q % 2 == 0 else nc.scalar
+            queue.dma_start(out=out_2[0, 4 * q : 4 * q + 4, :].bitcast(I32), in_=y_scales[32 * q : 32 * q + 4, :].bitcast(I32))

@@ -29,60 +29,50 @@ def tile_picked_ysubtr_sub_po_kernel(tc, x_words, x_scales, wc, ws, unit, vc, vs
         psum = ctx.enter_context(tc.psum_pool(name="psum", bufs=1))
 
         xs = keep.tile([P, T], U8, name="xs", align_bytes=64)
-        nc.gpsimd.memset(xs[:].bitcast(I32), 0)
+        nc.vector.memset(xs[:].bitcast(I32), 0)
+        xs_rows = keep.tile([P, T // 4], I32, name="xs_rows")
+        for q in range(4):
+            nc.sync.dma_start(out=xs_rows[32 * q : 32 * q + 4, :], in_=x_scales[0, 4 * q : 4 * q + 4, :].bitcast(I32))
         offsets = keep.tile([P, S // 16], U16, name="offsets")
         nc.sync.dma_start(offsets[:], offs)
         xw = keep.tile([P, T], I32, name="xw", align_bytes=64)
         nc.sync.dma_start(out=xw[:], in_=x_words[0].rearrange("p n t -> p (n t)").bitcast(I32))
         for q in range(4):
-            nc.scalar.dma_start(out=xs[32 * q : 32 * q + 4, :].bitcast(I32), in_=x_scales[0, 4 * q : 4 * q + 4, :].bitcast(I32))
+            nc.vector.tensor_copy(out=xs[32 * q : 32 * q + 4, :].bitcast(I32), in_=xs_rows[32 * q : 32 * q + 4, :])
 
-        warm = keep.tile([P, 2], F32, name="warm")
+        warm = keep.tile([P, PACK], F32, name="warm", tag="small")
         nc.gpsimd.memset(warm[:, 0:1], 1.0)
         nc.scalar.activation(warm[:, 1:2], warm[:, 0:1], ACT.Abs_reciprocal_sqrt)
 
-        def load(w, name, slot):
+        def load_whole(w, name):
+            raw = keep.tile([P, PACK, N], F32, name=f"{name}_raw", tag="whole")
+            nc.sync.dma_start(out=raw[:], in_=w.rearrange("(p j) c -> p j c", j=PACK))
+            return [raw[:, :, h * HALF : (h + 1) * HALF] for h in range(2)]
+
+        def load_halves(w, name):
             halves = []
             for h in range(2):
-                raw = keep.tile([P, PACK, HALF], F32, name=f"{name}_raw{h}", tag=f"raw{slot}{h}")
+                raw = keep.tile([P, PACK, HALF], F32, name=f"{name}_raw{h}", tag=f"half{h}")
                 nc.sync.dma_start(out=raw[:], in_=w.rearrange("(p j) c -> p j c", j=PACK)[:, :, h * HALF : (h + 1) * HALF])
-                halves.append(raw)
+                halves.append(raw[:])
             return halves
 
-        wc_raw = load(wc, "wc", 0)
-        ws_raw = load(ws, "ws", 1)
-        unit_sb = keep.tile([P, PACK], F32, name="unit_sb")
-        nc.gpsimd.dma_start(out=unit_sb[:], in_=unit.rearrange("(p t) o -> p (t o)", t=PACK))
+        wc_raw = load_whole(wc, "wc")
+        ws_raw = load_halves(ws, "ws")
+        unit_sb = keep.tile([P, PACK], F32, name="unit_sb", tag="small")
+        nc.sync.dma_start(out=unit_sb[:], in_=unit.rearrange("(p t) o -> p (t o)", t=PACK))
 
         xg = keep.tile([P, S], U32, name="xg", align_bytes=64)
         xgs = keep.tile([P, S], U8, name="xgs", align_bytes=64)
         nc.vector.tensor_copy(xg[:], xw[:].bitcast(U32).indirect(offsets[:]))
         nc.vector.tensor_copy(xgs[:], xs[:].indirect(offsets[:]))
 
-        def deal(copy, grouped, raws, part):
-            h, m0 = part // 2, 32 * (part % 2)
+        def deal(copy, grouped, raws, m0, m1):
+            h = m0 // 64
             copy(
-                out=grouped[:, :, 32 * part : 32 * (part + 1), :].rearrange("p t m j -> p m j t"),
-                in_=raws[h][:].rearrange("p j (m t) -> p m j t", t=PACK)[:, m0 : m0 + 32, :, :],
+                out=grouped[:, :, m0:m1, :].rearrange("p t m j -> p m j t"),
+                in_=raws[h].rearrange("p j (m t) -> p m j t", t=PACK)[:, m0 - 64 * h : m1 - 64 * h, :, :],
             )
-
-        def forward_weights(name, raws, copies):
-            codes = keep.tile([P, PACK, P], U32, name=f"{name}_codes", align_bytes=64)
-            scales = keep.tile([P, PACK, P], U8, name=f"{name}_scales", align_bytes=64)
-            for h in range(2):
-                grouped = keep.tile([P, PACK, 64, PACK], BF16, name=f"{name}_g{h}", align_bytes=64)
-                for u in range(2):
-                    copies[2 * h + u](
-                        out=grouped[:, :, 32 * u : 32 * (u + 1), :].rearrange("p t m j -> p m j t"),
-                        in_=raws[h][:].rearrange("p j (m t) -> p m j t", t=PACK)[:, 32 * u : 32 * (u + 1), :, :],
-                    )
-                for t in range(PACK):
-                    nc.vector.quantize_mx(
-                        out=codes[:, t, 64 * h : 64 * (h + 1)].bitcast(FP8X4),
-                        scales=scales[:, t, 64 * h : 64 * (h + 1)],
-                        in_=grouped[:, t, :, :].rearrange("p m j -> p (m j)"),
-                    )
-            return codes[:].rearrange("p t m -> p (t m)"), scales[:].rearrange("p t m -> p (t m)")
 
         def quantise(name, grouped):
             codes = keep.tile([P, N], U32, name=f"{name}_codes", align_bytes=64)
@@ -90,10 +80,10 @@ def tile_picked_ysubtr_sub_po_kernel(tc, x_words, x_scales, wc, ws, unit, vc, vs
             nc.vector.quantize_mx(out=codes[:].bitcast(FP8X4), scales=scales[:], in_=grouped[:].rearrange("p t m j -> p (t m j)"))
             return codes[:], scales[:]
 
-        def product(bank, t, weights, codes, scales, start, stop):
+        def product(out, t, weights, codes, scales, start, stop):
             cols = slice(t * P, (t + 1) * P)
             nc.tensor.matmul_mx(
-                out=bank[:, t, :],
+                out=out,
                 lhsT=weights[0][:, cols].bitcast(FP8X4),
                 lhsT_scale=weights[1][:, cols],
                 rhs=codes.bitcast(FP8X4),
@@ -103,23 +93,30 @@ def tile_picked_ysubtr_sub_po_kernel(tc, x_words, x_scales, wc, ws, unit, vc, vs
             )
 
         on_v, on_s = nc.vector.tensor_copy, nc.scalar.copy
-        wc_q = forward_weights("wc", wc_raw, (on_s, on_v, on_s, on_v))
+        wc_g = keep.tile([P, PACK, P, PACK], BF16, name="wc_g", align_bytes=64)
+        deal(on_s, wc_g, wc_raw, 0, 44)
+        deal(on_v, wc_g, wc_raw, 44, 64)
+        deal(on_v, wc_g, wc_raw, 64, 128)
+        wc_q = quantise("wc", wc_g)
+        ws_g = keep.tile([P, PACK, P, PACK], BF16, name="ws_g", align_bytes=64)
+        deal(on_s, ws_g, ws_raw, 0, 64)
 
         re, re2 = [], []
         for c in range(NCH):
             cols = slice(c * CH, (c + 1) * CH)
             bank = psum.tile([P, PACK, CH], F32, name=f"re{c}", tag=f"a{c}")
             for t in range(PACK):
-                product(bank, t, wc_q, xg[:, cols], xgs[:, cols], True, True)
+                product(bank[:, t, :], t, wc_q, xg[:, cols], xgs[:, cols], True, True)
             sq = keep.tile([P, PACK * CH], F32, name=f"re2_{c}")
             nc.scalar.activation(sq[:], bank[:].rearrange("p t j -> p (t j)"), ACT.Square)
             re.append(bank)
             re2.append(sq)
 
-        ws_q = forward_weights("ws", ws_raw, (on_v, on_v, on_v, on_v))
+        deal(on_v, ws_g, ws_raw, 64, 128)
+        ws_q = quantise("ws", ws_g)
 
-        vc_raw = load(vc, "vc", 0)
-        vs_raw = load(vs, "vs", 1)
+        vc_raw = load_whole(vc, "vc")
+        vs_raw = load_halves(vs, "vs")
 
         im, pw, least, inv, floor2, gain, zq = {}, {}, {}, {}, {}, {}, {}
 
@@ -127,7 +124,7 @@ def tile_picked_ysubtr_sub_po_kernel(tc, x_words, x_scales, wc, ws, unit, vc, vs
             cols = slice(c * CH, (c + 1) * CH)
             im[c] = psum.tile([P, PACK, CH], F32, name=f"im{c}", tag=f"b{c}")
             for t in range(PACK):
-                product(im[c], t, ws_q, xg[:, cols], xgs[:, cols], True, True)
+                product(im[c][:, t, :], t, ws_q, xg[:, cols], xgs[:, cols], True, True)
             im2 = keep.tile([P, PACK * CH], F32, name=f"im2_{c}")
             nc.scalar.activation(im2[:], im[c][:].rearrange("p t j -> p (t j)"), ACT.Square)
             pw[c] = keep.tile([P, PACK * CH], F32, name=f"pw{c}")
@@ -165,20 +162,26 @@ def tile_picked_ysubtr_sub_po_kernel(tc, x_words, x_scales, wc, ws, unit, vc, vs
 
         def hidden(c):
             z = keep.tile([P, 2, CH, PACK], BF16, name=f"z{c}", align_bytes=64)
-            for u, bank in enumerate((re[c], im[c])):
-                nc.vector.tensor_tensor(
-                    z[:, u, :, :].rearrange("p (a i) t -> p a t i", i=4),
-                    bank[:].rearrange("p t (a i) -> p a t i", i=4),
-                    gain[c][:].rearrange("p t (a i) -> p a t i", i=4),
-                    ALU.mult,
-                )
             codes = keep.tile([P, 2, CH], U32, name=f"z_codes{c}", align_bytes=64)
             scales = keep.tile([P, 2, CH], U8, name=f"z_scales{c}", align_bytes=64)
-            nc.vector.quantize_mx(
-                out=codes[:].rearrange("p u j -> p (u j)").bitcast(FP8X4),
-                scales=scales[:].rearrange("p u j -> p (u j)"),
-                in_=z[:].rearrange("p u j t -> p (u j t)"),
-            )
+            for u, bank in enumerate((re[c], im[c])):
+                nc.vector.tensor_tensor(
+                    z[:, u, :, :].rearrange("p (a i) t -> p a t i", i=2),
+                    bank[:].rearrange("p t (a i) -> p a t i", i=2),
+                    gain[c][:].rearrange("p t (a i) -> p a t i", i=2),
+                    ALU.mult,
+                )
+            if c < NCH - 1:
+                nc.vector.quantize_mx(
+                    out=codes[:].rearrange("p u j -> p (u j)").bitcast(FP8X4),
+                    scales=scales[:].rearrange("p u j -> p (u j)"),
+                    in_=z[:].rearrange("p u j t -> p (u j t)"),
+                )
+            else:
+                for u in range(2):
+                    nc.vector.quantize_mx(
+                        out=codes[:, u, :].bitcast(FP8X4), scales=scales[:, u, :], in_=z[:, u, :, :].rearrange("p j t -> p (j t)")
+                    )
             zq[c] = (codes, scales)
 
         y_codes = keep.tile([P, S], U32, name="y_codes", align_bytes=64)
@@ -188,37 +191,61 @@ def tile_picked_ysubtr_sub_po_kernel(tc, x_words, x_scales, wc, ws, unit, vc, vs
 
         def result(c, vc_q, vs_q):
             cols = slice(c * CH, (c + 1) * CH)
-            bank = psum.tile([P, PACK, CH], F32, name=f"y{c}", tag=f"a{c}")
             codes, scales = zq[c]
-            for t in range(PACK):
-                product(bank, t, vc_q, codes[:, 0, :], scales[:, 0, :], True, False)
-                product(bank, t, vs_q, codes[:, 1, :], scales[:, 1, :], False, True)
             y = keep.tile([P, PACK, CH], F32, name=f"y_sb{c}")
-            nc.scalar.copy(out=y[:], in_=bank[:])
-            nc.sync.dma_start(out=out_rows[:, :, cols], in_=y[:])
             y_g = keep.tile([P, CH, PACK], BF16, name=f"y_g{c}", align_bytes=64)
-            if c < NCH - 2:
-                on_s(out=y_g[:].rearrange("p (a i) t -> p a t i", i=4), in_=bank[:].rearrange("p t (a i) -> p a t i", i=4))
+            y_g_view = y_g[:].rearrange("p (a i) t -> p a t i", i=4)
+            if c < NCH - 1:
+                bank = psum.tile([P, PACK, CH], F32, name=f"y{c}", tag=f"a{c}")
+                for t in range(PACK):
+                    product(bank[:, t, :], t, vc_q, codes[:, 0, :], scales[:, 0, :], True, False)
+                    product(bank[:, t, :], t, vs_q, codes[:, 1, :], scales[:, 1, :], False, True)
+                nc.scalar.copy(out=y[:], in_=bank[:])
+                on_s(out=y_g_view, in_=bank[:].rearrange("p t (a i) -> p a t i", i=4))
             else:
-                on_v(out=y_g[:].rearrange("p (a i) t -> p a t i", i=4), in_=y[:].rearrange("p t (a i) -> p a t i", i=4))
+                banks = [psum.tile([P, CH], F32, name=f"y{c}_{t}", tag=tag) for t, tag in enumerate(("b0", "b1", "a0", "b2"))]
+                for t in range(PACK):
+                    product(banks[t][:], t, vc_q, codes[:, 0, :], scales[:, 0, :], True, False)
+                for t in range(PACK):
+                    product(banks[t][:], t, vs_q, codes[:, 1, :], scales[:, 1, :], False, True)
+                    nc.scalar.copy(out=y[:, t, :], in_=banks[t][:])
+                on_v(out=y_g_view, in_=y[:].rearrange("p t (a i) -> p a t i", i=4))
+            nc.sync.dma_start(out=out_rows[:, :, cols], in_=y[:])
             nc.vector.quantize_mx(out=y_codes[:, cols].bitcast(FP8X4), scales=y_scales[:, cols], in_=y_g[:].rearrange("p j t -> p (j t)"))
             nc.sync.dma_start(out=out_words[:, cols], in_=y_codes[:, cols].bitcast(I32))
 
         vc_g = keep.tile([P, PACK, P, PACK], BF16, name="vc_g", align_bytes=64)
         vs_g = keep.tile([P, PACK, P, PACK], BF16, name="vs_g", align_bytes=64)
-        stages = (power, noise, squared_gain, weighted_gain, hidden)
-        for step in range(NCH + len(stages) - 1):
-            for s in reversed(range(len(stages))):
-                if 0 <= step - s < NCH:
-                    stages[s](step - s)
+        power(0)
+        power(1)
+        noise(0)
+        noise(1)
+        power(2)
+        squared_gain(0)
+        noise(2)
+        power(3)
+        squared_gain(1)
+        weighted_gain(0)
+        noise(3)
+        hidden(0)
+        squared_gain(2)
+        weighted_gain(1)
         for part in range(4):
-            deal(on_s, vc_g, vc_raw, part)
+            deal(on_s, vc_g, vc_raw, 32 * part, 32 * (part + 1))
+        hidden(1)
+        squared_gain(3)
         vc_q = quantise("vc", vc_g)
         for part in range(4):
-            deal(on_s, vs_g, vs_raw, part)
+            deal(on_s, vs_g, vs_raw, 32 * part, 32 * (part + 1))
         vs_q = quantise("vs", vs_g)
-        for c in range(NCH):
-            result(c, vc_q, vs_q)
+        weighted_gain(2)
+        hidden(2)
+        result(0, vc_q, vs_q)
+        weighted_gain(3)
+        result(1, vc_q, vs_q)
+        hidden(3)
+        result(2, vc_q, vs_q)
+        result(3, vc_q, vs_q)
 
         for q in range(4):
             queue = nc.sync if q % 2 == 0 else nc.scalar

@@ -35,36 +35,35 @@ def tile_picked_ysubtr_sub_po_kernel(tc, x_words, x_scales, wc, ws, unit, vc, vs
             nc.sync.dma_start(out=xs_rows[32 * q : 32 * q + 4, :], in_=x_scales[0, 4 * q : 4 * q + 4, :].bitcast(I32))
         offsets = keep.tile([P, S // 16], U16, name="offsets")
         nc.sync.dma_start(offsets[:], offs)
-        xw = keep.tile([P, T], I32, name="xw", align_bytes=64)
-        nc.sync.dma_start(out=xw[:], in_=x_words[0].rearrange("p n t -> p (n t)").bitcast(I32))
         for q in range(4):
             nc.vector.tensor_copy(out=xs[32 * q : 32 * q + 4, :].bitcast(I32), in_=xs_rows[32 * q : 32 * q + 4, :])
 
-        warm = keep.tile([P, PACK], F32, name="warm", tag="small")
+        warm = keep.tile([P, PACK], F32, name="warm")
         nc.gpsimd.memset(warm[:, 0:1], 1.0)
         nc.scalar.activation(warm[:, 1:2], warm[:, 0:1], ACT.Abs_reciprocal_sqrt)
 
         def load_whole(w, name):
-            raw = keep.tile([P, PACK, N], F32, name=f"{name}_raw", tag="whole")
+            raw = keep.tile([P, PACK, N], F32, name=f"{name}_raw")
             nc.sync.dma_start(out=raw[:], in_=w.rearrange("(p j) c -> p j c", j=PACK))
             return [raw[:, :, h * HALF : (h + 1) * HALF] for h in range(2)]
 
         def load_halves(w, name):
             halves = []
             for h in range(2):
-                raw = keep.tile([P, PACK, HALF], F32, name=f"{name}_raw{h}", tag=f"half{h}")
+                raw = keep.tile([P, PACK, HALF], F32, name=f"{name}_raw{h}")
                 nc.sync.dma_start(out=raw[:], in_=w.rearrange("(p j) c -> p j c", j=PACK)[:, :, h * HALF : (h + 1) * HALF])
                 halves.append(raw[:])
             return halves
 
-        wc_raw = load_whole(wc, "wc")
+        wc_raw = load_halves(wc, "wc")
+        xw = keep.tile([P, T], I32, name="xw", align_bytes=64)
+        nc.sync.dma_start(out=xw[:], in_=x_words[0].rearrange("p n t -> p (n t)").bitcast(I32))
         ws_raw = load_halves(ws, "ws")
-        unit_sb = keep.tile([P, PACK], F32, name="unit_sb", tag="small")
+        unit_sb = keep.tile([P, PACK], F32, name="unit_sb")
         nc.sync.dma_start(out=unit_sb[:], in_=unit.rearrange("(p t) o -> p (t o)", t=PACK))
 
         xg = keep.tile([P, S], U32, name="xg", align_bytes=64)
         xgs = keep.tile([P, S], U8, name="xgs", align_bytes=64)
-        nc.vector.tensor_copy(xg[:], xw[:].bitcast(U32).indirect(offsets[:]))
         nc.vector.tensor_copy(xgs[:], xs[:].indirect(offsets[:]))
 
         def deal(copy, grouped, raws, m0, m1):
@@ -94,158 +93,204 @@ def tile_picked_ysubtr_sub_po_kernel(tc, x_words, x_scales, wc, ws, unit, vc, vs
 
         on_v, on_s = nc.vector.tensor_copy, nc.scalar.copy
         wc_g = keep.tile([P, PACK, P, PACK], BF16, name="wc_g", align_bytes=64)
-        deal(on_s, wc_g, wc_raw, 0, 44)
-        deal(on_v, wc_g, wc_raw, 44, 64)
-        deal(on_v, wc_g, wc_raw, 64, 128)
+        deal(on_s, wc_g, wc_raw, 0, 64)
+        deal(on_s, wc_g, wc_raw, 64, 84)
+        deal(on_v, wc_g, wc_raw, 84, 128)
         wc_q = quantise("wc", wc_g)
+        for h in range(2):
+            nc.vector.tensor_copy(xg[:, h * HALF : (h + 1) * HALF], xw[:].bitcast(U32).indirect(offsets[:, 16 * h : 16 * (h + 1)]))
         ws_g = keep.tile([P, PACK, P, PACK], BF16, name="ws_g", align_bytes=64)
-        deal(on_s, ws_g, ws_raw, 0, 64)
+        deal(on_v, ws_g, ws_raw, 0, 64)
 
-        re, re2 = [], []
+        re = []
         for c in range(NCH):
             cols = slice(c * CH, (c + 1) * CH)
             bank = psum.tile([P, PACK, CH], F32, name=f"re{c}", tag=f"a{c}")
             for t in range(PACK):
                 product(bank[:, t, :], t, wc_q, xg[:, cols], xgs[:, cols], True, True)
-            sq = keep.tile([P, PACK * CH], F32, name=f"re2_{c}")
-            nc.scalar.activation(sq[:], bank[:].rearrange("p t j -> p (t j)"), ACT.Square)
             re.append(bank)
-            re2.append(sq)
 
         deal(on_v, ws_g, ws_raw, 64, 128)
         ws_q = quantise("ws", ws_g)
 
-        vc_raw = load_whole(vc, "vc")
-        vs_raw = load_halves(vs, "vs")
+        vc_raw = load_halves(vc, "vc")
+        vs_raw = load_whole(vs, "vs")
 
-        im, pw, least, inv, floor2, gain, zq = {}, {}, {}, {}, {}, {}, {}
+        def flat(tile):
+            return tile[:].rearrange("p t j -> p (t j)")
 
-        def power(c):
+        def chunk_tiles(name):
+            return [keep.tile([P, PACK, CH], F32, name=f"{name}{c}") for c in range(NCH)]
+
+        re2, im2, pw, root, inv, ratio, gain2, inv_gain, gain = [
+            chunk_tiles(name) for name in ("re2_", "im2_", "pw", "root", "inv", "ratio", "gain2_", "inv_gain", "gain")
+        ]
+        least = [keep.tile([P, PACK * CH // D], F32, name=f"least{c}") for c in range(NCH)]
+        z = [keep.tile([P, 2, CH, PACK], BF16, name=f"z{c}", align_bytes=64) for c in range(NCH)]
+        z_codes = [keep.tile([P, 2, CH], U32, name=f"z_codes{c}", align_bytes=64) for c in range(NCH)]
+        z_scales = [keep.tile([P, 2, CH], U8, name=f"z_scales{c}", align_bytes=64) for c in range(NCH)]
+
+        for c in range(NCH):
+            nc.scalar.activation(flat(re2[c]), flat(re[c]), ACT.Square)
+        im = []
+        for c in range(NCH):
             cols = slice(c * CH, (c + 1) * CH)
-            im[c] = psum.tile([P, PACK, CH], F32, name=f"im{c}", tag=f"b{c}")
+            bank = psum.tile([P, PACK, CH], F32, name=f"im{c}", tag=f"b{c}")
             for t in range(PACK):
-                product(im[c][:, t, :], t, ws_q, xg[:, cols], xgs[:, cols], True, True)
-            im2 = keep.tile([P, PACK * CH], F32, name=f"im2_{c}")
-            nc.scalar.activation(im2[:], im[c][:].rearrange("p t j -> p (t j)"), ACT.Square)
-            pw[c] = keep.tile([P, PACK * CH], F32, name=f"pw{c}")
-            nc.vector.tensor_tensor(pw[c][:], re2[c][:], im2[:], ALU.add)
+                product(bank[:, t, :], t, ws_q, xg[:, cols], xgs[:, cols], True, True)
+            im.append(bank)
 
-        def noise(c):
-            least[c] = keep.tile([P, PACK * CH // D], F32, name=f"least{c}")
-            nc.vector.tensor_reduce(least[c][:], pw[c][:].rearrange("p (v d) -> p v d", d=D), mybir.AxisListType.X, ALU.min)
-            root = keep.tile([P, PACK * CH], F32, name=f"root{c}")
-            nc.scalar.activation(root[:], pw[c][:], ACT.Abs_reciprocal_sqrt, bias=0.05)
-            inv[c] = keep.tile([P, PACK * CH], F32, name=f"inv{c}")
-            nc.scalar.activation(inv[c][:], root[:], ACT.Square)
+        def groups(tile):
+            return tile[:].rearrange("p t (v d) -> p (t v) d", d=D)
 
-        def squared_gain(c):
-            ratio = keep.tile([P, PACK * CH // D, D], F32, name=f"ratio{c}")
-            nc.vector.scalar_tensor_tensor(
-                ratio[:],
-                inv[c][:].rearrange("p (v d) -> p v d", d=D),
-                -1.5,
-                least[c][:].unsqueeze(2).broadcast_to([P, PACK * CH // D, D]),
-                ALU.mult,
-                ALU.mult,
-            )
-            floor2[c] = keep.tile([P, PACK, CH], F32, name=f"g2_{c}")
-            nc.vector.tensor_scalar(
-                floor2[c][:].rearrange("p t j -> p (t j)"), ratio[:].rearrange("p v d -> p (v d)"), 1.02, 0.02, ALU.add, ALU.max
-            )
+        def square_im(c):
+            nc.scalar.activation(flat(im2[c]), flat(im[c]), ACT.Square)
+
+        def add_power(c):
+            nc.vector.tensor_tensor(flat(pw[c]), flat(re2[c]), flat(im2[c]), ALU.add)
+
+        def least_power(c):
+            nc.vector.tensor_reduce(least[c][:], groups(pw[c]), mybir.AxisListType.X, ALU.min)
+
+        def inverse_root(c):
+            nc.scalar.activation(flat(root[c]), flat(pw[c]), ACT.Abs_reciprocal_sqrt, bias=0.05)
+
+        def inverse(c):
+            nc.scalar.activation(flat(inv[c]), flat(root[c]), ACT.Square)
+
+        def noise_ratio(c):
+            spread = least[c][:].unsqueeze(2).broadcast_to([P, PACK * CH // D, D])
+            nc.vector.scalar_tensor_tensor(groups(ratio[c]), groups(inv[c]), -1.5, spread, ALU.mult, ALU.mult)
+
+        def clamp(c):
+            nc.vector.tensor_scalar(flat(gain2[c]), flat(ratio[c]), 1.02, 0.02, ALU.add, ALU.max)
+
+        def inverse_gain(c):
+            nc.scalar.activation(flat(inv_gain[c]), flat(gain2[c]), ACT.Abs_reciprocal_sqrt)
 
         def weighted_gain(c):
-            rs = keep.tile([P, PACK, CH], F32, name=f"rs{c}")
-            nc.scalar.activation(rs[:], floor2[c][:], ACT.Abs_reciprocal_sqrt)
-            gain[c] = keep.tile([P, PACK, CH], F32, name=f"gain{c}")
             for t in range(PACK):
-                nc.vector.scalar_tensor_tensor(gain[c][:, t, :], floor2[c][:, t, :], unit_sb[:, t : t + 1], rs[:, t, :], ALU.mult, ALU.mult)
+                nc.vector.scalar_tensor_tensor(
+                    gain[c][:, t, :], gain2[c][:, t, :], unit_sb[:, t : t + 1], inv_gain[c][:, t, :], ALU.mult, ALU.mult
+                )
 
         def hidden(c):
-            z = keep.tile([P, 2, CH, PACK], BF16, name=f"z{c}", align_bytes=64)
-            codes = keep.tile([P, 2, CH], U32, name=f"z_codes{c}", align_bytes=64)
-            scales = keep.tile([P, 2, CH], U8, name=f"z_scales{c}", align_bytes=64)
             for u, bank in enumerate((re[c], im[c])):
                 nc.vector.tensor_tensor(
-                    z[:, u, :, :].rearrange("p (a i) t -> p a t i", i=2),
+                    z[c][:, u, :, :].rearrange("p (a i) t -> p a t i", i=2),
                     bank[:].rearrange("p t (a i) -> p a t i", i=2),
                     gain[c][:].rearrange("p t (a i) -> p a t i", i=2),
                     ALU.mult,
                 )
-            if c < NCH - 1:
-                nc.vector.quantize_mx(
-                    out=codes[:].rearrange("p u j -> p (u j)").bitcast(FP8X4),
-                    scales=scales[:].rearrange("p u j -> p (u j)"),
-                    in_=z[:].rearrange("p u j t -> p (u j t)"),
-                )
-            else:
-                for u in range(2):
-                    nc.vector.quantize_mx(
-                        out=codes[:, u, :].bitcast(FP8X4), scales=scales[:, u, :], in_=z[:, u, :, :].rearrange("p j t -> p (j t)")
-                    )
-            zq[c] = (codes, scales)
+
+        def quantise_hidden(c, u0, u1):
+            nc.vector.quantize_mx(
+                out=z_codes[c][:, u0:u1, :].rearrange("p u j -> p (u j)").bitcast(FP8X4),
+                scales=z_scales[c][:, u0:u1, :].rearrange("p u j -> p (u j)"),
+                in_=z[c][:, u0:u1, :, :].rearrange("p u j t -> p (u j t)"),
+            )
 
         y_codes = keep.tile([P, S], U32, name="y_codes", align_bytes=64)
         y_scales = keep.tile([P, S], U8, name="y_scales", align_bytes=64)
         out_rows = out_0.rearrange("(p t) j -> p t j", t=PACK)
         out_words = out_1[0].rearrange("p n t -> p (n t)").bitcast(I32)
 
-        def result(c, vc_q, vs_q):
-            cols = slice(c * CH, (c + 1) * CH)
-            codes, scales = zq[c]
-            y = keep.tile([P, PACK, CH], F32, name=f"y_sb{c}")
-            y_g = keep.tile([P, CH, PACK], BF16, name=f"y_g{c}", align_bytes=64)
-            y_g_view = y_g[:].rearrange("p (a i) t -> p a t i", i=4)
-            if c < NCH - 1:
-                bank = psum.tile([P, PACK, CH], F32, name=f"y{c}", tag=f"a{c}")
-                for t in range(PACK):
-                    product(bank[:, t, :], t, vc_q, codes[:, 0, :], scales[:, 0, :], True, False)
-                    product(bank[:, t, :], t, vs_q, codes[:, 1, :], scales[:, 1, :], False, True)
-                nc.scalar.copy(out=y[:], in_=bank[:])
-                on_s(out=y_g_view, in_=bank[:].rearrange("p t (a i) -> p a t i", i=4))
-            else:
-                banks = [psum.tile([P, CH], F32, name=f"y{c}_{t}", tag=tag) for t, tag in enumerate(("b0", "b1", "a0", "b2"))]
-                for t in range(PACK):
-                    product(banks[t][:], t, vc_q, codes[:, 0, :], scales[:, 0, :], True, False)
-                for t in range(PACK):
-                    product(banks[t][:], t, vs_q, codes[:, 1, :], scales[:, 1, :], False, True)
-                    nc.scalar.copy(out=y[:, t, :], in_=banks[t][:])
-                on_v(out=y_g_view, in_=y[:].rearrange("p t (a i) -> p a t i", i=4))
-            nc.sync.dma_start(out=out_rows[:, :, cols], in_=y[:])
-            nc.vector.quantize_mx(out=y_codes[:, cols].bitcast(FP8X4), scales=y_scales[:, cols], in_=y_g[:].rearrange("p j t -> p (j t)"))
-            nc.sync.dma_start(out=out_words[:, cols], in_=y_codes[:, cols].bitcast(I32))
-
+        y = chunk_tiles("y")
+        y_g = [keep.tile([P, CH, PACK], BF16, name=f"y_g{c}", align_bytes=64) for c in range(NCH)]
         vc_g = keep.tile([P, PACK, P, PACK], BF16, name="vc_g", align_bytes=64)
         vs_g = keep.tile([P, PACK, P, PACK], BF16, name="vs_g", align_bytes=64)
-        power(0)
-        power(1)
-        noise(0)
-        noise(1)
-        power(2)
-        squared_gain(0)
-        noise(2)
-        power(3)
-        squared_gain(1)
+
+        def store_result(c):
+            nc.sync.dma_start(out=out_rows[:, :, c * CH : (c + 1) * CH], in_=y[c][:])
+
+        def result(c, round_too):
+            bank = psum.tile([P, PACK, CH], F32, name=f"y_bank{c}", tag=f"a{c}")
+            for t in range(PACK):
+                product(bank[:, t, :], t, vc_q, z_codes[c][:, 0, :], z_scales[c][:, 0, :], True, False)
+                product(bank[:, t, :], t, vs_q, z_codes[c][:, 1, :], z_scales[c][:, 1, :], False, True)
+            nc.scalar.copy(out=y[c][:], in_=bank[:])
+            store_result(c)
+            if round_too:
+                nc.scalar.copy(out=y_g[c][:], in_=bank[:].rearrange("p t j -> p j t"))
+
+        def round_result(c):
+            nc.vector.tensor_copy(out=y_g[c][:].rearrange("p (a i) t -> p a t i", i=4), in_=y[c][:].rearrange("p t (a i) -> p a t i", i=4))
+
+        def quantise_result(c):
+            cols = slice(c * CH, (c + 1) * CH)
+            nc.vector.quantize_mx(out=y_codes[:, cols].bitcast(FP8X4), scales=y_scales[:, cols], in_=y_g[c][:].rearrange("p j t -> p (j t)"))
+
+        deal(on_v, vc_g, vc_raw, 0, 44)
+        square_im(0)
+        square_im(1)
+        add_power(0)
+        add_power(1)
+        inverse_root(0)
+        square_im(2)
+        inverse(0)
+        least_power(0)
+        least_power(1)
+        add_power(2)
+        inverse_root(1)
+        square_im(3)
+        inverse(1)
+        noise_ratio(0)
+        least_power(2)
+        clamp(0)
+        add_power(3)
+        noise_ratio(1)
+        inverse_root(2)
+        inverse_gain(0)
+        inverse(2)
+        least_power(3)
+        clamp(1)
+        inverse_root(3)
+        inverse_gain(1)
+        inverse(3)
+        for m0, m1 in ((44, 64), (64, 96), (96, 128)):
+            deal(on_s, vc_g, vc_raw, m0, m1)
         weighted_gain(0)
-        noise(3)
+        noise_ratio(2)
         hidden(0)
-        squared_gain(2)
-        weighted_gain(1)
-        for part in range(4):
-            deal(on_s, vc_g, vc_raw, 32 * part, 32 * (part + 1))
-        hidden(1)
-        squared_gain(3)
+        clamp(2)
+        inverse_gain(2)
+        quantise_hidden(0, 0, 2)
         vc_q = quantise("vc", vc_g)
+        weighted_gain(1)
+        noise_ratio(3)
+        hidden(1)
+        clamp(3)
         for part in range(4):
             deal(on_s, vs_g, vs_raw, 32 * part, 32 * (part + 1))
+        inverse_gain(3)
         vs_q = quantise("vs", vs_g)
+        result(0, True)
         weighted_gain(2)
+        quantise_hidden(1, 0, 2)
+        result(1, True)
         hidden(2)
-        result(0, vc_q, vs_q)
         weighted_gain(3)
-        result(1, vc_q, vs_q)
+        quantise_hidden(2, 0, 2)
+        result(2, False)
         hidden(3)
-        result(2, vc_q, vs_q)
-        result(3, vc_q, vs_q)
+        quantise_hidden(3, 0, 1)
+        quantise_result(0)
+        quantise_hidden(3, 1, 2)
+        last = NCH - 1
+        banks = [psum.tile([P, CH], F32, name=f"y_last{t}", tag=tag) for t, tag in enumerate(("b0", "b1", "b2", "a0"))]
+        for t in range(PACK):
+            product(banks[t][:], t, vc_q, z_codes[last][:, 0, :], z_scales[last][:, 0, :], True, False)
+        for t in range(PACK):
+            product(banks[t][:], t, vs_q, z_codes[last][:, 1, :], z_scales[last][:, 1, :], False, True)
+            nc.scalar.copy(out=y[last][:, t, :], in_=banks[t][:])
+        store_result(last)
+        round_result(2)
+        quantise_result(1)
+        quantise_result(2)
+        nc.sync.dma_start(out=out_words[:, : last * CH], in_=y_codes[:, : last * CH].bitcast(I32))
+        round_result(last)
+        quantise_result(last)
+        nc.sync.dma_start(out=out_words[:, last * CH :], in_=y_codes[:, last * CH :].bitcast(I32))
 
         for q in range(4):
             queue = nc.sync if q % 2 == 0 else nc.scalar

from contextlib import ExitStack

import concourse.mybir as mybir

K, T, S, D, H, N = 512, 1024, 512, 8, 512, 512
FLOPS = 4 * 2 * 512 * 512 * 512

F32 = mybir.dt.float32
BF16 = mybir.dt.bfloat16
I32 = mybir.dt.int32
U32 = mybir.dt.uint32
U16 = mybir.dt.uint16
U8 = mybir.dt.uint8
FP8X4 = mybir.dt.float8_e4m3fn_x4
ALU = mybir.AluOpType
ACT = mybir.ActivationFunctionType

P = 128
PACK = 4
CH = 128
NCH = S // CH
HALF = 256


def tile_picked_ysubtr_sub_po_kernel(tc, x_words, x_scales, wc, ws, unit, vc, vs, offs, out_0, out_1, out_2):
    nc = tc.nc
    with ExitStack() as ctx:
        keep = ctx.enter_context(tc.tile_pool(name="keep", bufs=1))
        psum = ctx.enter_context(tc.psum_pool(name="psum", bufs=1))

        xs = keep.tile([P, T], U8, name="xs", align_bytes=64)
        nc.vector.memset(xs[:].bitcast(I32), 0)
        xs_rows = keep.tile([P, T // 4], I32, name="xs_rows")
        for q in range(4):
            nc.sync.dma_start(out=xs_rows[32 * q : 32 * q + 4, :], in_=x_scales[0, 4 * q : 4 * q + 4, :].bitcast(I32))
        offsets = keep.tile([P, S // 16], U16, name="offsets")
        nc.sync.dma_start(offsets[:], offs)
        for q in range(4):
            nc.vector.tensor_copy(out=xs[32 * q : 32 * q + 4, :].bitcast(I32), in_=xs_rows[32 * q : 32 * q + 4, :])

        warm = keep.tile([P, PACK], F32, name="warm")
        nc.gpsimd.memset(warm[:, 0:1], 1.0)
        nc.scalar.activation(warm[:, 1:2], warm[:, 0:1], ACT.Abs_reciprocal_sqrt)

        def load_whole(w, name):
            raw = keep.tile([P, PACK, N], F32, name=f"{name}_raw")
            nc.sync.dma_start(out=raw[:], in_=w.rearrange("(p j) c -> p j c", j=PACK))
            return [raw[:, :, h * HALF : (h + 1) * HALF] for h in range(2)]

        def load_halves(w, name):
            halves = []
            for h in range(2):
                raw = keep.tile([P, PACK, HALF], F32, name=f"{name}_raw{h}")
                nc.sync.dma_start(out=raw[:], in_=w.rearrange("(p j) c -> p j c", j=PACK)[:, :, h * HALF : (h + 1) * HALF])
                halves.append(raw[:])
            return halves

        wc_raw = load_halves(wc, "wc")
        xw = keep.tile([P, T], I32, name="xw", align_bytes=64)
        nc.sync.dma_start(out=xw[:], in_=x_words[0].rearrange("p n t -> p (n t)").bitcast(I32))
        ws_raw = load_halves(ws, "ws")
        unit_sb = keep.tile([P, PACK], F32, name="unit_sb")
        nc.sync.dma_start(out=unit_sb[:], in_=unit.rearrange("(p t) o -> p (t o)", t=PACK))

        xg = keep.tile([P, S], U32, name="xg", align_bytes=64)
        xgs = keep.tile([P, S], U8, name="xgs", align_bytes=64)
        nc.vector.tensor_copy(xgs[:], xs[:].indirect(offsets[:]))

        def deal(copy, grouped, raws, m0, m1):
            h = m0 // 64
            copy(
                out=grouped[:, :, m0:m1, :].rearrange("p t m j -> p m j t"),
                in_=raws[h].rearrange("p j (m t) -> p m j t", t=PACK)[:, m0 - 64 * h : m1 - 64 * h, :, :],
            )

        def quantise(name, grouped):
            codes = keep.tile([P, N], U32, name=f"{name}_codes", align_bytes=64)
            scales = keep.tile([P, N], U8, name=f"{name}_scales", align_bytes=64)
            nc.vector.quantize_mx(out=codes[:].bitcast(FP8X4), scales=scales[:], in_=grouped[:].rearrange("p t m j -> p (t m j)"))
            return codes[:], scales[:]

        def product(out, t, weights, codes, scales, start, stop):
            cols = slice(t * P, (t + 1) * P)
            nc.tensor.matmul_mx(
                out=out,
                lhsT=weights[0][:, cols].bitcast(FP8X4),
                lhsT_scale=weights[1][:, cols],
                rhs=codes.bitcast(FP8X4),
                rhs_scale=scales,
                start=start,
                stop=stop,
            )

        on_v, on_s = nc.vector.tensor_copy, nc.scalar.copy
        wc_g = keep.tile([P, PACK, P, PACK], BF16, name="wc_g", align_bytes=64)
        deal(on_s, wc_g, wc_raw, 0, 64)
        deal(on_s, wc_g, wc_raw, 64, 84)
        deal(on_v, wc_g, wc_raw, 84, 128)
        wc_q = quantise("wc", wc_g)
        for h in range(2):
            nc.vector.tensor_copy(xg[:, h * HALF : (h + 1) * HALF], xw[:].bitcast(U32).indirect(offsets[:, 16 * h : 16 * (h + 1)]))
        ws_g = keep.tile([P, PACK, P, PACK], BF16, name="ws_g", align_bytes=64)
        deal(on_v, ws_g, ws_raw, 0, 64)

        re = []
        for c in range(NCH):
            cols = slice(c * CH, (c + 1) * CH)
            bank = psum.tile([P, PACK, CH], F32, name=f"re{c}", tag=f"a{c}")
            for t in range(PACK):
                product(bank[:, t, :], t, wc_q, xg[:, cols], xgs[:, cols], True, True)
            re.append(bank)

        deal(on_v, ws_g, ws_raw, 64, 128)
        ws_q = quantise("ws", ws_g)

        vc_raw = load_halves(vc, "vc")
        vs_raw = load_whole(vs, "vs")

        def flat(tile):
            return tile[:].rearrange("p t j -> p (t j)")

        def chunk_tiles(name):
            return [keep.tile([P, PACK, CH], F32, name=f"{name}{c}") for c in range(NCH)]

        re2, im2, pw, root, inv, ratio, gain2, inv_gain, gain = [
            chunk_tiles(name) for name in ("re2_", "im2_", "pw", "root", "inv", "ratio", "gain2_", "inv_gain", "gain")
        ]
        least = [keep.tile([P, PACK * CH // D], F32, name=f"least{c}") for c in range(NCH)]
        z = [keep.tile([P, 2, CH, PACK], BF16, name=f"z{c}", align_bytes=64) for c in range(NCH)]
        z_codes = [keep.tile([P, 2, CH], U32, name=f"z_codes{c}", align_bytes=64) for c in range(NCH)]
        z_scales = [keep.tile([P, 2, CH], U8, name=f"z_scales{c}", align_bytes=64) for c in range(NCH)]

        for c in range(NCH):
            nc.scalar.activation(flat(re2[c]), flat(re[c]), ACT.Square)
        im = []
        for c in range(NCH):
            cols = slice(c * CH, (c + 1) * CH)
            bank = psum.tile([P, PACK, CH], F32, name=f"im{c}", tag=f"b{c}")
            for t in range(PACK):
                product(bank[:, t, :], t, ws_q, xg[:, cols], xgs[:, cols], True, True)
            im.append(bank)

        def groups(tile):
            return tile[:].rearrange("p t (v d) -> p (t v) d", d=D)

        def square_im(c):
            nc.scalar.activation(flat(im2[c]), flat(im[c]), ACT.Square)

        def add_power(c):
            nc.vector.tensor_tensor(flat(pw[c]), flat(re2[c]), flat(im2[c]), ALU.add)

        def least_power(c):
            nc.vector.tensor_reduce(least[c][:], groups(pw[c]), mybir.AxisListType.X, ALU.min)

        def inverse_root(c):
            nc.scalar.activation(flat(root[c]), flat(pw[c]), ACT.Abs_reciprocal_sqrt, bias=0.05)

        def inverse(c):
            nc.scalar.activation(flat(inv[c]), flat(root[c]), ACT.Square)

        def noise_ratio(c):
            spread = least[c][:].unsqueeze(2).broadcast_to([P, PACK * CH // D, D])
            nc.vector.scalar_tensor_tensor(groups(ratio[c]), groups(inv[c]), -1.5, spread, ALU.mult, ALU.mult)

        def clamp(c):
            nc.vector.tensor_scalar(flat(gain2[c]), flat(ratio[c]), 1.02, 0.02, ALU.add, ALU.max)

        def inverse_gain(c):
            nc.scalar.activation(flat(inv_gain[c]), flat(gain2[c]), ACT.Abs_reciprocal_sqrt)

        def weighted_gain(c):
            for t in range(PACK):
                nc.vector.scalar_tensor_tensor(
                    gain[c][:, t, :], gain2[c][:, t, :], unit_sb[:, t : t + 1], inv_gain[c][:, t, :], ALU.mult, ALU.mult
                )

        def hidden(c):
            for u, bank in enumerate((re[c], im[c])):
                nc.vector.tensor_tensor(
                    z[c][:, u, :, :].rearrange("p (a i) t -> p a t i", i=2),
                    bank[:].rearrange("p t (a i) -> p a t i", i=2),
                    gain[c][:].rearrange("p t (a i) -> p a t i", i=2),
                    ALU.mult,
                )

        def quantise_hidden(c, u0, u1):
            nc.vector.quantize_mx(
                out=z_codes[c][:, u0:u1, :].rearrange("p u j -> p (u j)").bitcast(FP8X4),
                scales=z_scales[c][:, u0:u1, :].rearrange("p u j -> p (u j)"),
                in_=z[c][:, u0:u1, :, :].rearrange("p u j t -> p (u j t)"),
            )

        y_codes = keep.tile([P, S], U32, name="y_codes", align_bytes=64)
        y_scales = keep.tile([P, S], U8, name="y_scales", align_bytes=64)
        out_rows = out_0.rearrange("(p t) j -> p t j", t=PACK)
        out_words = out_1[0].rearrange("p n t -> p (n t)").bitcast(I32)

        y = chunk_tiles("y")
        y_g = [keep.tile([P, CH, PACK], BF16, name=f"y_g{c}", align_bytes=64) for c in range(NCH)]
        vc_g = keep.tile([P, PACK, P, PACK], BF16, name="vc_g", align_bytes=64)
        vs_g = keep.tile([P, PACK, P, PACK], BF16, name="vs_g", align_bytes=64)

        def store_result(c):
            nc.sync.dma_start(out=out_rows[:, :, c * CH : (c + 1) * CH], in_=y[c][:])

        def result(c, round_too):
            bank = psum.tile([P, PACK, CH], F32, name=f"y_bank{c}", tag=f"a{c}")
            for t in range(PACK):
                product(bank[:, t, :], t, vc_q, z_codes[c][:, 0, :], z_scales[c][:, 0, :], True, False)
                product(bank[:, t, :], t, vs_q, z_codes[c][:, 1, :], z_scales[c][:, 1, :], False, True)
            nc.scalar.copy(out=y[c][:], in_=bank[:])
            store_result(c)
            if round_too:
                nc.scalar.copy(out=y_g[c][:], in_=bank[:].rearrange("p t j -> p j t"))

        def round_result(c):
            nc.vector.tensor_copy(out=y_g[c][:].rearrange("p (a i) t -> p a t i", i=4), in_=y[c][:].rearrange("p t (a i) -> p a t i", i=4))

        def quantise_result(c):
            cols = slice(c * CH, (c + 1) * CH)
            nc.vector.quantize_mx(out=y_codes[:, cols].bitcast(FP8X4), scales=y_scales[:, cols], in_=y_g[c][:].rearrange("p j t -> p (j t)"))

        deal(on_v, vc_g, vc_raw, 0, 44)
        square_im(0)
        square_im(1)
        add_power(0)
        add_power(1)
        inverse_root(0)
        square_im(2)
        inverse(0)
        least_power(0)
        least_power(1)
        add_power(2)
        inverse_root(1)
        square_im(3)
        inverse(1)
        noise_ratio(0)
        least_power(2)
        clamp(0)
        add_power(3)
        noise_ratio(1)
        inverse_root(2)
        inverse_gain(0)
        inverse(2)
        least_power(3)
        clamp(1)
        inverse_root(3)
        inverse_gain(1)
        inverse(3)
        for m0, m1 in ((44, 64), (64, 96), (96, 128)):
            deal(on_s, vc_g, vc_raw, m0, m1)
        weighted_gain(0)
        noise_ratio(2)
        hidden(0)
        clamp(2)
        inverse_gain(2)
        quantise_hidden(0, 0, 2)
        vc_q = quantise("vc", vc_g)
        weighted_gain(1)
        noise_ratio(3)
        hidden(1)
        clamp(3)
        for part in range(4):
            deal(on_s, vs_g, vs_raw, 32 * part, 32 * (part + 1))
        inverse_gain(3)
        vs_q = quantise("vs", vs_g)
        result(0, True)
        weighted_gain(2)
        quantise_hidden(1, 0, 2)
        result(1, True)
        hidden(2)
        weighted_gain(3)
        quantise_hidden(2, 0, 2)
        result(2, False)
        hidden(3)
        quantise_hidden(3, 0, 1)
        quantise_result(0)
        quantise_hidden(3, 1, 2)
        last = NCH - 1
        banks = [psum.tile([P, CH], F32, name=f"y_last{t}", tag=tag) for t, tag in enumerate(("b0", "b1", "b2", "a0"))]
        for t in range(PACK):
            product(banks[t][:], t, vc_q, z_codes[last][:, 0, :], z_scales[last][:, 0, :], True, False)
        for t in range(PACK):
            product(banks[t][:], t, vs_q, z_codes[last][:, 1, :], z_scales[last][:, 1, :], False, True)
            nc.scalar.copy(out=y[last][:, t, :], in_=banks[t][:])
        store_result(last)
        round_result(2)
        quantise_result(1)
        quantise_result(2)
        nc.sync.dma_start(out=out_words[:, : last * CH], in_=y_codes[:, : last * CH].bitcast(I32))
        round_result(last)
        quantise_result(last)
        nc.sync.dma_start(out=out_words[:, last * CH :], in_=y_codes[:, last * CH :].bitcast(I32))

        for q in range(4):
            queue = nc.sync if q % 2 == 0 else nc.scalar
            queue.dma_start(out=out_2[0, 4 * q : 4 * q + 4, :].bitcast(I32), in_=y_scales[32 * q : 32 * q + 4, :].bitcast(I32))
